import numpy as np
import ml_dtypes


def mxq(x, axis, fmt="e4m3"):
    dtype, down = {"e4m3": (ml_dtypes.float8_e4m3fn, 7), "e5m2": (ml_dtypes.float8_e5m2, 14)}[fmt]
    v = np.moveaxis(np.asarray(x, np.float32).astype(ml_dtypes.bfloat16).astype(np.float64), axis, -1)
    blocks = v.reshape(v.shape[:-1] + (-1, 32))
    amax = np.abs(blocks).max(-1, keepdims=True)
    byte = np.maximum(np.where(amax > 0, np.frexp(amax)[1] - 1 + 127, 0) - down, 1)
    scale = np.exp2(byte - 127.0)
    codes = (blocks / scale).astype(np.float32).astype(dtype).astype(np.float64)
    return np.moveaxis((codes * scale).reshape(v.shape), -1, axis)


WIDE = False


def mx_kscale(k):
    if not WIDE:
        return np.ones(k)
    levels = np.array([10, -10, 5, -5, 0])
    if k % 512:
        return np.exp2(np.random.permutation(np.resize(levels, k // 32))).repeat(32)
    a = np.empty((k // 512, 16))
    for p in range(k // 512):
        a[p, :8] = np.random.permutation(np.resize(levels, 8))
        for g in range(8):
            far = levels[np.abs(levels - a[p, g]) >= 10]
            a[p, g + 8] = far[np.random.randint(len(far))]
    return np.exp2(a.ravel()).repeat(32)


def f64(x):
    return np.asarray(x).astype(np.float64)


def striped(idx):
    return np.tile(idx.reshape(-1, 16).T, (8, 1)).astype(np.uint16)


def unstriped(offs):
    return offs[:16].T.reshape(-1).astype(np.int64)


def striped8(idx):
    return np.concatenate([x.reshape(-1, 16).T for x in idx]).astype(np.uint16)


def runs(offs, k):
    lists = np.stack([offs[16 * r : 16 * r + 16].T.reshape(-1) for r in range(8)]).astype(np.int64)
    return lists[np.arange(k) % 512 // 64]


def pack_weight(w):
    k, n = w.shape
    w = f64(np.asarray(w, np.float32).astype(ml_dtypes.bfloat16)).reshape(k // 32, 32, n)
    amax = np.abs(w).max(1)
    byte = np.clip(np.where(amax > 0, np.frexp(amax)[1] - 1 + 127 - 7, 1), 1, 254)
    scaled = (w * np.exp2(127.0 - byte)[:, None, :]).reshape(k, n).astype(np.float32)
    words = np.ascontiguousarray(scaled.reshape(k // 512, 128, 4, n).transpose(0, 1, 3, 2)).astype(ml_dtypes.float8_e4m3fn).view(np.uint8)
    return words, np.ascontiguousarray(byte.astype(np.uint8).reshape(k // 512, 16, n))


def unpack_weight(words, scales):
    g, p, n, _ = words.shape
    vals = np.ascontiguousarray(words).view(ml_dtypes.float8_e4m3fn).astype(np.float64) * np.repeat(np.exp2(scales.astype(np.float64) - 127.0), 8, axis=1)[..., None]
    return vals.transpose(0, 1, 3, 2).reshape(g * 512, n)


def sigmoid(v):
    return 1.0 / (1.0 + np.exp(-np.maximum(v, -700.0)))


K, T, S, V, H, J = 512, 2048, 512, 512, 512, 512


def setup_inputs():
    n = np.random.standard_normal
    s = mx_kscale(K)[:, None]
    u = mx_kscale(S)
    packed_xT = pack_weight(n((K, T)) * s)
    return {
        "x_words": packed_xT[0],
        "x_scales": packed_xT[1],
        "w1": (n((K, H)) / np.sqrt(K) / s).astype(np.float32),
        "w2": (n((K, H)) / np.sqrt(K) / s).astype(np.float32),
        "tab": np.random.uniform(0.4, 1.4, (H, J)).astype(np.float32),
        "ga": (np.random.uniform(0.5, 1.5, (H, 1)) * u[:, None]).astype(np.float32),
        "gb": (np.random.uniform(0.5, 1.5, (H, 1)) / u[:, None]).astype(np.float32),
        "offs": striped8(np.random.randint(0, T, (8, S))),
        "two": striped(np.random.permutation(T)[:V]),
        "n1": striped8(np.stack([np.random.permutation(S) for _ in range(8)])),
        "n2": striped8(np.random.randint(0, J, (8, V))),
        "n3": striped8(np.stack([np.random.permutation(V) for _ in range(8)])),
        "n4": striped8(np.stack([np.random.permutation(V) for _ in range(8)])),
        "n5": striped8(np.stack([np.random.permutation(V) for _ in range(8)])),
    }


def reference(x_words, x_scales, w1, w2, tab, ga, gb, offs, two, n1, n2, n3, n4, n5):
    xq = unpack_weight(x_words, x_scales)[np.arange(K)[:, None], runs(offs, K)]
    a = mxq(f64(w1), 0, "e4m3").T @ xq
    st = a * (sigmoid(a[np.arange(H)[:, None], runs(n1, H)]))
    z = f64(ga) * (np.maximum(st, st[np.arange(H)[:, None], runs(n1, H)]))
    x_two = unpack_weight(x_words, x_scales)[:, unstriped(two)]
    b = mxq(f64(w2), 0, "e4m3").T @ x_two
    z2 = f64(gb) * (b * (f64(tab)[np.arange(H)[:, None], runs(n2, H)]) - (0.5 * (b[np.arange(H)[:, None], runs(n3, H)])))
    s = 0.0625 * ((mxq(z, 0, "e4m3").T @ mxq(z2, 0, "e4m3")))
    return np.maximum(s[np.arange(S)[:, None], runs(n4, S)], s[np.arange(S)[:, None], runs(n5, S)]) - (0.75 * s)

@@ -1,0 +1,215 @@
+from contextlib import ExitStack
+
+import concourse.mybir as mybir
+
+K, T, S = 512, 2048, 512
+FLOPS = 3 * 2 * 512 * 512 * 512
+
+F32 = mybir.dt.float32
+BF16 = mybir.dt.bfloat16
+I32 = mybir.dt.int32
+U32 = mybir.dt.uint32
+U16 = mybir.dt.uint16
+U8 = mybir.dt.uint8
+FP8X4 = mybir.dt.float8_e4m3fn_x4
+ALU = mybir.AluOpType
+ACT = mybir.ActivationFunctionType
+
+P = 128
+N = 512
+HALF = N // 2
+LIST_COLS = N // 16
+
+
+def tile_picked_hkqtwicpkindgover_none_p_kernel(tc, x_words, x_scales, w1, w2, tab, ga, gb, offs, two, n1, n2, n3, n4, n5, out):
+    nc = tc.nc
+    with ExitStack() as ctx:
+        held = ctx.enter_context(tc.tile_pool(name="held", bufs=1))
+        psum = ctx.enter_context(tc.psum_pool(name="psum", bufs=1))
+
+        def sb(name, shape, dtype):
+            return held.tile(shape, dtype, name=name, align_bytes=64)
+
+        def four(name, shape, dtype):
+            return [sb("%s%d" % (name, t), shape, dtype) for t in range(4)]
+
+        def dealt(rows):
+            return rows.rearrange("(p t) c -> t p c", t=4)
+
+        lists = {}
+
+        def load_lists(*named):
+            for name, src in named:
+                lists[name] = held.tile([P, LIST_COLS], U16, name="list_" + name)
+                nc.sync.dma_start(lists[name][:], src)
+
+        def look(window, name, h):
+            return window[:].indirect(lists[name][:, h * (LIST_COLS // 2) : (h + 1) * (LIST_COLS // 2)])
+
+        def cols(h):
+            return slice(h * HALF, (h + 1) * HALF)
+
+        scale_table = sb("scale_table", [P, T], U8)
+        nc.vector.memset(scale_table[:].bitcast(I32), 0)
+        scale_rows = x_scales[0].bitcast(I32)
+        table_i32 = scale_table[:].bitcast(I32)
+        nc.scalar.dma_start(table_i32[0:P:8, :], scale_rows)
+        for r in (1, 2, 3):
+            nc.scalar.dma_start(table_i32[r:P:32, :], scale_rows[r:16:4, :])
+
+        word_table = sb("word_table", [P, T], U32)
+        nc.sync.dma_start(word_table[:].bitcast(I32), x_words[0].rearrange("p c r -> p (c r)").bitcast(I32))
+        load_lists(("two", two), ("offs", offs))
+        w2_raw = sb("w2_raw", [P, 4, N], F32)
+        nc.sync.dma_start(w2_raw[:], w2.rearrange("(p j) c -> p j c", j=4))
+        load_lists(("n3", n3), ("n2", n2), ("n1", n1))
+        tabs = four("tab", [P, N], F32)
+        for t in range(4):
+            nc.sync.dma_start(tabs[t][:], dealt(tab)[t])
+
+        w1_raw = sb("w1_raw", [P, 4, N], F32)
+        nc.sync.dma_start(w1_raw[:], w1.rearrange("(p j) c -> p j c", j=4))
+        load_lists(("n4", n4), ("n5", n5))
+
+        ga_raw = sb("ga_raw", [P, 4], F32)
+        gb_raw = sb("gb_raw", [P, 4], F32)
+        nc.scalar.dma_start(ga_raw[:], ga.rearrange("(p t) o -> p (t o)", t=4))
+        nc.scalar.dma_start(gb_raw[:], gb.rearrange("(p t) o -> p (t o)", t=4))
+        nonneg = sb("nonneg", [P, 4], F32)
+        sign = sb("sign", [P, 4], F32)
+        ga_abs = sb("ga_abs", [P, 4], F32)
+        gb_signed = sb("gb_signed", [P, 4], F32)
+        nc.vector.tensor_scalar(nonneg[:], ga_raw[:], 0.0, 2.0, ALU.is_ge, ALU.mult)
+        nc.vector.tensor_scalar(sign[:], nonneg[:], -1.0, None, ALU.add)
+        nc.vector.tensor_tensor(gb_signed[:], gb_raw[:], sign[:], ALU.mult)
+        nc.vector.tensor_tensor(ga_abs[:], ga_raw[:], sign[:], ALU.mult)
+
+        two_words = sb("two_words", [P, N], U32)
+        offs_words = sb("offs_words", [P, N], U32)
+        nc.vector.tensor_copy(two_words[:], word_table[:].indirect(lists["two"][:]))
+        nc.vector.tensor_copy(offs_words[:], word_table[:].indirect(lists["offs"][:]))
+
+        two_scales = sb("two_scales", [P, N], U8)
+        offs_bytes = sb("offs_bytes", [P, N], U8)
+        offs_scales = sb("offs_scales", [P, N], U8)
+        nc.vector.tensor_copy(two_scales[:], scale_table[:].indirect(lists["two"][:]))
+        nc.vector.tensor_copy(offs_bytes[:], scale_table[:].indirect(lists["offs"][:]))
+        nc.vector.tensor_copy(offs_scales[:].bitcast(I32), offs_bytes[:].bitcast(I32))
+        for r in (2, 3):
+            nc.sync.dma_start(offs_scales[:].bitcast(I32)[r:P:32, :], offs_bytes[:].bitcast(I32)[8 * r : P : 32, :])
+
+        def deal_copy(engine, dst, src, u):
+            o = dst[:].rearrange("p e (m j) -> p m j e", j=4)
+            s = src[:].rearrange("p j (m u e) -> p u m j e", u=2, e=2)[:, u]
+            if engine == "vector":
+                nc.vector.tensor_copy(o, s)
+            else:
+                nc.scalar.copy(o, s)
+
+        def quantise(name, grouped, width):
+            codes = sb(name + "_codes", [P, width], U32)
+            scales = sb(name + "_scales", [P, width], U8)
+            nc.vector.quantize_mx(out=codes[:].bitcast(FP8X4), scales=scales[:], in_=grouped)
+            return codes, scales
+
+        def product(bank, stationary, moving):
+            acc = psum.tile([P, N], F32, name=bank, tag=bank)
+            nc.tensor.matmul_mx(
+                out=acc[:],
+                lhsT=stationary[0][:].bitcast(FP8X4),
+                lhsT_scale=stationary[1][:],
+                rhs=moving[0][:].bitcast(FP8X4),
+                rhs_scale=moving[1][:],
+                start=True,
+                stop=True,
+            )
+            return acc
+
+        def pairs(name):
+            return [sb("%s%d" % (name, u), [P, 2, N], BF16) for u in range(2)]
+
+        w2_grouped = pairs("w2_grouped")
+        w1_grouped = pairs("w1_grouped")
+        deal_copy("scalar", w2_grouped[0], w2_raw, 0)
+        deal_copy("scalar", w2_grouped[1], w2_raw, 1)
+        b_acc = []
+        for t in range(4):
+            b_acc.append(product("bank%d" % t, quantise("w2_%d" % t, w2_grouped[t // 2][:, t % 2, :], P), (two_words, two_scales)))
+
+        b_win = four("b_win", [P, N], F32)
+        nc.scalar.activation(b_win[0][:], b_acc[0][:], ACT.Copy, scale=gb_signed[:, 0:1])
+        for t in (1, 2, 3):
+            nc.vector.tensor_scalar(b_win[t][:], b_acc[t][:], gb_signed[:, t : t + 1], None, ALU.mult)
+
+        for u in range(2):
+            deal_copy("vector", w1_grouped[u], w1_raw, u)
+        a_acc = []
+        for t in range(4):
+            a_acc.append(product("bank%d" % (4 + t), quantise("w1_%d" % t, w1_grouped[t // 2][:, t % 2, :], P), (offs_words, offs_scales)))
+
+        a_win = four("a_win", [P, N], F32)
+        gate = four("gate", [P, N], F32)
+        st_win = four("st_win", [P, N], F32)
+        st_far = four("st_far", [P, N], F32)
+        kind_term = sb("kind_term", [P, 4, N], F32)
+        far_term = sb("far_term", [P, 4, N], F32)
+        larger = sb("larger", [P, 4, N], F32)
+
+        def b_step(t):
+            for h in range(2):
+                nc.scalar.activation(far_term[:, t, cols(h)], look(b_win[t], "n3", h), ACT.Copy, scale=-0.5)
+            for h in range(2):
+                nc.vector.tensor_tensor(kind_term[:, t, cols(h)], look(tabs[t], "n2", h), b_win[t][:, cols(h)], ALU.mult)
+
+        def a_front(t):
+            nc.scalar.copy(a_win[t][:], a_acc[t][:])
+            for h in range(2):
+                nc.scalar.activation(gate[t][:, cols(h)], look(a_win[t], "n1", h), ACT.Sigmoid)
+            nc.vector.scalar_tensor_tensor(st_win[t][:], a_acc[t][:], ga_abs[:, t : t + 1], gate[t][:], ALU.mult, ALU.mult)
+
+        def a_back(t):
+            for h in range(2):
+                nc.scalar.activation(st_far[t][:, cols(h)], look(st_win[t], "n1", h), ACT.Copy)
+            nc.vector.tensor_tensor(larger[:, t, :], st_win[t][:], st_far[t][:], ALU.max)
+
+        for t in range(4):
+            b_step(t)
+            a_front(t)
+            if t >= 1:
+                a_back(t - 1)
+
+        z2_grouped = sb("z2_grouped", [P, N, 4], BF16)
+        for h in range(2):
+            nc.vector.tensor_tensor(
+                z2_grouped[:, cols(h), :].rearrange("p (c i) t -> p c t i", i=2),
+                kind_term[:, :, cols(h)].rearrange("p t (c i) -> p c t i", i=2),
+                far_term[:, :, cols(h)].rearrange("p t (c i) -> p c t i", i=2),
+                ALU.add,
+            )
+        z2_q = quantise("z2", z2_grouped[:].rearrange("p c t -> p (c t)"), N)
+        a_back(3)
+
+        z_grouped = pairs("z_grouped")
+        deal_copy("vector", z_grouped[0], larger, 0)
+        deal_copy("scalar", z_grouped[1], larger, 1)
+        s_acc = []
+        for t in range(4):
+            s_acc.append(product("bank%d" % t, quantise("z_%d" % t, z_grouped[t // 2][:, t % 2, :], P), z2_q))
+
+        s_win = four("s_win", [P, N], F32)
+        at_n4 = four("at_n4", [P, N], F32)
+        at_n5 = four("at_n5", [P, N], F32)
+        top = four("top", [P, N], F32)
+        result = four("result", [P, N], F32)
+        for t in range(4):
+            nc.scalar.activation(s_win[t][:], s_acc[t][:], ACT.Copy, scale=0.0625)
+            for h in range(2):
+                nc.scalar.activation(at_n4[t][:, cols(h)], look(s_win[t], "n4", h), ACT.Copy)
+            for h in range(2):
+                if h == 1 and t % 2 == 1:
+                    nc.scalar.activation(at_n5[t][:, cols(h)], look(s_win[t], "n5", h), ACT.Copy)
+                else:
+                    nc.vector.tensor_copy(at_n5[t][:, cols(h)], look(s_win[t], "n5", h))
+            nc.vector.tensor_tensor(top[t][:], at_n4[t][:], at_n5[t][:], ALU.max)
+            nc.vector.scalar_tensor_tensor(result[t][:], s_win[t][:], -0.75, top[t][:], ALU.mult, ALU.add)
+            nc.sync.dma_start(dealt(out)[t], result[t][:])

@@ -2,7 +2,7 @@ from contextlib import ExitStack
 
 import concourse.mybir as mybir
 
-K, T, S = 512, 2048, 512
+T = 2048
 FLOPS = 3 * 2 * 512 * 512 * 512
 
 F32 = mybir.dt.float32
@@ -33,73 +33,32 @@ def tile_picked_hkqtwicpkindgover_none_p_kernel(tc, x_words, x_scales, w1, w2, t
         def four(name, shape, dtype):
             return [sb("%s%d" % (name, t), shape, dtype) for t in range(4)]
 
+        def pairs(name):
+            return [sb("%s%d" % (name, u), [P, 2, N], BF16) for u in range(2)]
+
         def dealt(rows):
             return rows.rearrange("(p t) c -> t p c", t=4)
 
         lists = {}
 
-        def load_lists(*named):
-            for name, src in named:
-                lists[name] = held.tile([P, LIST_COLS], U16, name="list_" + name)
-                nc.sync.dma_start(lists[name][:], src)
-
-        def look(window, name, h):
-            return window[:].indirect(lists[name][:, h * (LIST_COLS // 2) : (h + 1) * (LIST_COLS // 2)])
+        def load_list(name, src):
+            lists[name] = held.tile([P, LIST_COLS], U16, name="list_" + name)
+            nc.sync.dma_start(lists[name][:], src)
 
         def cols(h):
             return slice(h * HALF, (h + 1) * HALF)
 
-        scale_table = sb("scale_table", [P, T], U8)
-        nc.vector.memset(scale_table[:].bitcast(I32), 0)
-        scale_rows = x_scales[0].bitcast(I32)
-        table_i32 = scale_table[:].bitcast(I32)
-        nc.scalar.dma_start(table_i32[0:P:8, :], scale_rows)
-        for r in (1, 2, 3):
-            nc.scalar.dma_start(table_i32[r:P:32, :], scale_rows[r:16:4, :])
+        def look(window, name, h):
+            return window[:].indirect(lists[name][:, h * (LIST_COLS // 2) : (h + 1) * (LIST_COLS // 2)])
 
-        word_table = sb("word_table", [P, T], U32)
-        nc.sync.dma_start(word_table[:].bitcast(I32), x_words[0].rearrange("p c r -> p (c r)").bitcast(I32))
-        load_lists(("two", two), ("offs", offs))
-        w2_raw = sb("w2_raw", [P, 4, N], F32)
-        nc.sync.dma_start(w2_raw[:], w2.rearrange("(p j) c -> p j c", j=4))
-        load_lists(("n3", n3), ("n2", n2), ("n1", n1))
-        tabs = four("tab", [P, N], F32)
-        for t in range(4):
-            nc.sync.dma_start(tabs[t][:], dealt(tab)[t])
-
-        w1_raw = sb("w1_raw", [P, 4, N], F32)
-        nc.sync.dma_start(w1_raw[:], w1.rearrange("(p j) c -> p j c", j=4))
-        load_lists(("n4", n4), ("n5", n5))
-
-        ga_raw = sb("ga_raw", [P, 4], F32)
-        gb_raw = sb("gb_raw", [P, 4], F32)
-        nc.scalar.dma_start(ga_raw[:], ga.rearrange("(p t) o -> p (t o)", t=4))
-        nc.scalar.dma_start(gb_raw[:], gb.rearrange("(p t) o -> p (t o)", t=4))
-        nonneg = sb("nonneg", [P, 4], F32)
-        sign = sb("sign", [P, 4], F32)
-        ga_abs = sb("ga_abs", [P, 4], F32)
-        gb_signed = sb("gb_signed", [P, 4], F32)
-        nc.vector.tensor_scalar(nonneg[:], ga_raw[:], 0.0, 2.0, ALU.is_ge, ALU.mult)
-        nc.vector.tensor_scalar(sign[:], nonneg[:], -1.0, None, ALU.add)
-        nc.vector.tensor_tensor(gb_signed[:], gb_raw[:], sign[:], ALU.mult)
-        nc.vector.tensor_tensor(ga_abs[:], ga_raw[:], sign[:], ALU.mult)
-
-        two_words = sb("two_words", [P, N], U32)
-        offs_words = sb("offs_words", [P, N], U32)
-        nc.vector.tensor_copy(two_words[:], word_table[:].indirect(lists["two"][:]))
-        nc.vector.tensor_copy(offs_words[:], word_table[:].indirect(lists["offs"][:]))
-
-        two_scales = sb("two_scales", [P, N], U8)
-        offs_bytes = sb("offs_bytes", [P, N], U8)
-        offs_scales = sb("offs_scales", [P, N], U8)
-        nc.vector.tensor_copy(two_scales[:], scale_table[:].indirect(lists["two"][:]))
-        nc.vector.tensor_copy(offs_bytes[:], scale_table[:].indirect(lists["offs"][:]))
-        nc.vector.tensor_copy(offs_scales[:].bitcast(I32), offs_bytes[:].bitcast(I32))
-        for r in (2, 3):
-            nc.sync.dma_start(offs_scales[:].bitcast(I32)[r:P:32, :], offs_bytes[:].bitcast(I32)[8 * r : P : 32, :])
+        def fetch(engine, dst, window, name, h):
+            if engine == "vector":
+                nc.vector.tensor_copy(dst[:, cols(h)], look(window, name, h))
+            else:
+                nc.scalar.activation(dst[:, cols(h)], look(window, name, h), ACT.Copy)
 
         def deal_copy(engine, dst, src, u):
-            o = dst[:].rearrange("p e (m j) -> p m j e", j=4)
+            o = dst.rearrange("p e (m j) -> p m j e", j=4)
             s = src[:].rearrange("p j (m u e) -> p u m j e", u=2, e=2)[:, u]
             if engine == "vector":
                 nc.vector.tensor_copy(o, s)
@@ -125,28 +84,80 @@ def tile_picked_hkqtwicpkindgover_none_p_kernel(tc, x_words, x_scales, w1, w2, t
             )
             return acc
 
-        def pairs(name):
-            return [sb("%s%d" % (name, u), [P, 2, N], BF16) for u in range(2)]
+        warm_in = sb("warm_in", [P, 1], F32)
+        warm_out = sb("warm_out", [P, 1], F32)
+        nc.vector.memset(warm_in[:], 0.0)
+        nc.scalar.activation(warm_out[:], warm_in[:], ACT.Sigmoid)
 
+        scale_table = sb("scale_table", [P, T], U8)
+        table_i32 = scale_table[:].bitcast(I32)
+        nc.gpsimd.memset(table_i32, 0)
+        scale_rows = x_scales[0].bitcast(I32)
+
+        def load_scales():
+            nc.sync.dma_start(table_i32[0:P:8, :], scale_rows)
+            for r in (1, 2, 3):
+                nc.sync.dma_start(table_i32[r:P:32, :], scale_rows[r:16:4, :])
+
+        word_table = sb("word_table", [P, T], U32)
+        w2_raw = [sb("w2_raw%d" % h, [P, 4, HALF], F32) for h in range(2)]
+        ga_raw = sb("ga_raw", [P, 4], F32)
+        gb_raw = sb("gb_raw", [P, 4], F32)
+        w1_raw = sb("w1_raw", [P, 4, N], F32)
+        tabs = four("tab", [P, N], F32)
+
+        def load_tab(t):
+            nc.sync.dma_start(tabs[t][:], dealt(tab)[t])
+
+        def load_w(dst, w):
+            nc.sync.dma_start(dst[:], w.rearrange("(p j) c -> p j c", j=4))
+
+        def load_w2():
+            for h in range(2):
+                load_w(w2_raw[h], w2[:, cols(h)])
+
+        def load_gains():
+            nc.sync.dma_start(ga_raw[:], ga.rearrange("(p t) o -> p (t o)", t=4))
+            nc.sync.dma_start(gb_raw[:], gb.rearrange("(p t) o -> p (t o)", t=4))
+
+        def load_words():
+            nc.sync.dma_start(word_table[:].bitcast(I32), x_words[0].rearrange("p c r -> p (c r)").bitcast(I32))
+
+        load_list("two", two)
+        load_list("offs", offs)
+        load_scales()
+        load_words()
+        load_gains()
+        load_w2()
+        load_list("n3", n3)
+        load_w(w1_raw, w1)
+        load_list("n2", n2)
+        load_tab(0)
+        load_tab(1)
+        load_list("n1", n1)
+        load_tab(2)
+        load_tab(3)
+        load_list("n4", n4)
+        load_list("n5", n5)
+
+        half_sign = sb("half_sign", [P, 4], F32)
+        ga_half = sb("ga_half", [P, 4], F32)
+        gb_half = sb("gb_half", [P, 4], F32)
+
+        def signs():
+            nc.vector.tensor_scalar(half_sign[:], ga_raw[:], 0.0, -0.5, ALU.is_ge, ALU.add)
+            nc.vector.tensor_tensor(gb_half[:], gb_raw[:], half_sign[:], ALU.mult)
+            nc.vector.tensor_tensor(ga_half[:], ga_raw[:], half_sign[:], ALU.mult)
+
+        two_scales = sb("two_scales", [P, N], U8)
+        offs_bytes = sb("offs_bytes", [P, N], U8)
+        offs_scales = sb("offs_scales", [P, N], U8)
+        two_words = sb("two_words", [P, N], U32)
+        offs_words = sb("offs_words", [P, N], U32)
         w2_grouped = pairs("w2_grouped")
         w1_grouped = pairs("w1_grouped")
-        deal_copy("scalar", w2_grouped[0], w2_raw, 0)
-        deal_copy("scalar", w2_grouped[1], w2_raw, 1)
-        b_acc = []
-        for t in range(4):
-            b_acc.append(product("bank%d" % t, quantise("w2_%d" % t, w2_grouped[t // 2][:, t % 2, :], P), (two_words, two_scales)))
-
+        z_grouped = pairs("z_grouped")
         b_win = four("b_win", [P, N], F32)
-        nc.scalar.activation(b_win[0][:], b_acc[0][:], ACT.Copy, scale=gb_signed[:, 0:1])
-        for t in (1, 2, 3):
-            nc.vector.tensor_scalar(b_win[t][:], b_acc[t][:], gb_signed[:, t : t + 1], None, ALU.mult)
-
-        for u in range(2):
-            deal_copy("vector", w1_grouped[u], w1_raw, u)
-        a_acc = []
-        for t in range(4):
-            a_acc.append(product("bank%d" % (4 + t), quantise("w1_%d" % t, w1_grouped[t // 2][:, t % 2, :], P), (offs_words, offs_scales)))
-
         a_win = four("a_win", [P, N], F32)
         gate = four("gate", [P, N], F32)
         st_win = four("st_win", [P, N], F32)
@@ -154,62 +165,172 @@ def tile_picked_hkqtwicpkindgover_none_p_kernel(tc, x_words, x_scales, w1, w2, t
         kind_term = sb("kind_term", [P, 4, N], F32)
         far_term = sb("far_term", [P, 4, N], F32)
         larger = sb("larger", [P, 4, N], F32)
+        z2_grouped = sb("z2_grouped", [P, N, 4], BF16)
+        s_win = four("s_win", [P, N], F32)
+        at_n4 = four("at_n4", [P, N], F32)
+        at_n5 = four("at_n5", [P, N], F32)
+        top = four("top", [P, N], F32)
+        result = four("result", [P, N], F32)
+        acc = {}
+        q = {}
 
-        def b_step(t):
+        def gather_packed(dst, table, name):
+            nc.vector.tensor_copy(dst[:], table[:].indirect(lists[name][:]))
+
+        def place_scales():
+            nc.vector.tensor_copy(offs_scales[:].bitcast(I32), offs_bytes[:].bitcast(I32))
+            for r in (2, 3):
+                nc.scalar.dma_start(offs_scales[:].bitcast(I32)[r:P:32, :], offs_bytes[:].bitcast(I32)[8 * r : P : 32, :])
+
+        def b_product(t):
+            acc["b", t] = product("bank%d" % t, quantise("w2_%d" % t, w2_grouped[t // 2][:, t % 2, :], P), (two_words, two_scales))
+
+        def a_product(t):
+            acc["a", t] = product("bank%d" % (4 + t), quantise("w1_%d" % t, w1_grouped[t // 2][:, t % 2, :], P), (offs_words, offs_scales))
+
+        def s_product(t):
+            acc["s", t] = product("bank%d" % t, quantise("z_%d" % t, z_grouped[t // 2][:, t % 2, :], P), q["z2"])
+
+        def b_out(engine, t):
+            if engine == "vector":
+                nc.vector.tensor_scalar(b_win[t][:], acc["b", t][:], gb_half[:, t : t + 1], None, ALU.mult)
+            else:
+                nc.scalar.activation(b_win[t][:], acc["b", t][:], ACT.Copy, scale=gb_half[:, t : t + 1])
+
+        def far_b(t):
             for h in range(2):
                 nc.scalar.activation(far_term[:, t, cols(h)], look(b_win[t], "n3", h), ACT.Copy, scale=-0.5)
+
+        def kind_b(t):
             for h in range(2):
                 nc.vector.tensor_tensor(kind_term[:, t, cols(h)], look(tabs[t], "n2", h), b_win[t][:, cols(h)], ALU.mult)
 
-        def a_front(t):
-            nc.scalar.copy(a_win[t][:], a_acc[t][:])
+        def a_out(engine, t):
+            if engine == "vector":
+                nc.vector.tensor_copy(a_win[t][:], acc["a", t][:])
+            else:
+                nc.scalar.copy(a_win[t][:], acc["a", t][:])
+
+        def gate_a(t):
             for h in range(2):
                 nc.scalar.activation(gate[t][:, cols(h)], look(a_win[t], "n1", h), ACT.Sigmoid)
-            nc.vector.scalar_tensor_tensor(st_win[t][:], a_acc[t][:], ga_abs[:, t : t + 1], gate[t][:], ALU.mult, ALU.mult)
 
-        def a_back(t):
+        def gated(t):
+            nc.vector.scalar_tensor_tensor(st_win[t][:], acc["a", t][:], ga_half[:, t : t + 1], gate[t][:], ALU.mult, ALU.mult)
+
+        def far_st(engines, t):
             for h in range(2):
-                nc.scalar.activation(st_far[t][:, cols(h)], look(st_win[t], "n1", h), ACT.Copy)
+                fetch(engines[h], st_far[t], st_win[t], "n1", h)
+
+        def take_larger(t):
             nc.vector.tensor_tensor(larger[:, t, :], st_win[t][:], st_far[t][:], ALU.max)
 
-        for t in range(4):
-            b_step(t)
-            a_front(t)
-            if t >= 1:
-                a_back(t - 1)
-
-        z2_grouped = sb("z2_grouped", [P, N, 4], BF16)
-        for h in range(2):
+        def z2_sum(h):
             nc.vector.tensor_tensor(
                 z2_grouped[:, cols(h), :].rearrange("p (c i) t -> p c t i", i=2),
                 kind_term[:, :, cols(h)].rearrange("p t (c i) -> p c t i", i=2),
                 far_term[:, :, cols(h)].rearrange("p t (c i) -> p c t i", i=2),
                 ALU.add,
             )
-        z2_q = quantise("z2", z2_grouped[:].rearrange("p c t -> p (c t)"), N)
-        a_back(3)
 
-        z_grouped = pairs("z_grouped")
-        deal_copy("vector", z_grouped[0], larger, 0)
-        deal_copy("scalar", z_grouped[1], larger, 1)
-        s_acc = []
-        for t in range(4):
-            s_acc.append(product("bank%d" % t, quantise("z_%d" % t, z_grouped[t // 2][:, t % 2, :], P), z2_q))
+        def z2_quantise():
+            q["z2"] = quantise("z2", z2_grouped[:].rearrange("p c t -> p (c t)"), N)
 
-        s_win = four("s_win", [P, N], F32)
-        at_n4 = four("at_n4", [P, N], F32)
-        at_n5 = four("at_n5", [P, N], F32)
-        top = four("top", [P, N], F32)
-        result = four("result", [P, N], F32)
-        for t in range(4):
-            nc.scalar.activation(s_win[t][:], s_acc[t][:], ACT.Copy, scale=0.0625)
-            for h in range(2):
-                nc.scalar.activation(at_n4[t][:, cols(h)], look(s_win[t], "n4", h), ACT.Copy)
-            for h in range(2):
-                if h == 1 and t % 2 == 1:
-                    nc.scalar.activation(at_n5[t][:, cols(h)], look(s_win[t], "n5", h), ACT.Copy)
-                else:
-                    nc.vector.tensor_copy(at_n5[t][:, cols(h)], look(s_win[t], "n5", h))
-            nc.vector.tensor_tensor(top[t][:], at_n4[t][:], at_n5[t][:], ALU.max)
-            nc.vector.scalar_tensor_tensor(result[t][:], s_win[t][:], -0.75, top[t][:], ALU.mult, ALU.add)
-            nc.sync.dma_start(dealt(out)[t], result[t][:])
+        def s_out(engine, t):
+            if engine == "vector":
+                nc.vector.tensor_scalar(s_win[t][:], acc["s", t][:], 0.25, None, ALU.mult)
+            else:
+                nc.scalar.activation(s_win[t][:], acc["s", t][:], ACT.Copy, scale=0.25)
+
+        def finish(t, c):
+            nc.vector.tensor_tensor(top[t][:, c], at_n4[t][:, c], at_n5[t][:, c], ALU.max)
+            nc.vector.scalar_tensor_tensor(result[t][:, c], s_win[t][:, c], -0.75, top[t][:, c], ALU.mult, ALU.add)
+            nc.sync.dma_start(dealt(out)[t][:, c], result[t][:, c])
+
+        V, S = "vector", "scalar"
+        gather_packed(two_scales, scale_table, "two")
+        gather_packed(offs_bytes, scale_table, "offs")
+        place_scales()
+        signs()
+        gather_packed(two_words, word_table, "two")
+        gather_packed(offs_words, word_table, "offs")
+        deal_copy(S, w2_grouped[0][:, :, cols(0)], w2_raw[0], 0)
+        deal_copy(S, w2_grouped[1][:, :, cols(0)], w2_raw[0], 1)
+        deal_copy(S, w2_grouped[0][:, :, cols(1)], w2_raw[1], 0)
+        deal_copy(S, w2_grouped[1][:, :, cols(1)], w2_raw[1], 1)
+        b_product(0)
+        b_product(1)
+        b_product(2)
+        b_product(3)
+        b_out(S, 0)
+        b_out(V, 1)
+        b_out(V, 2)
+        b_out(V, 3)
+        deal_copy(V, w1_grouped[0][:], w1_raw, 0)
+        deal_copy(V, w1_grouped[1][:], w1_raw, 1)
+        a_product(0)
+        a_product(1)
+        a_product(2)
+        a_product(3)
+        far_b(0)
+        far_b(1)
+        far_b(2)
+        far_b(3)
+        kind_b(0)
+        kind_b(1)
+        kind_b(2)
+        kind_b(3)
+        a_out(S, 0)
+        gate_a(0)
+        a_out(S, 1)
+        gate_a(1)
+        a_out(S, 2)
+        gate_a(2)
+        a_out(S, 3)
+        gate_a(3)
+        gated(0)
+        gated(1)
+        z2_sum(0)
+        z2_sum(1)
+        gated(2)
+        z2_quantise()
+        far_st((V, V), 0)
+        gated(3)
+        take_larger(0)
+        far_st((S, S), 1)
+        take_larger(1)
+        far_st((S, S), 2)
+        take_larger(2)
+        far_st((S, S), 3)
+        take_larger(3)
+        deal_copy(V, z_grouped[0][:], larger, 0)
+        deal_copy(S, z_grouped[1][:], larger, 1)
+        s_product(0)
+        s_product(1)
+        s_product(2)
+        s_product(3)
+        s_out(S, 0)
+        s_out(V, 1)
+        fetch(S, at_n4[0], s_win[0], "n4", 0)
+        fetch(S, at_n4[0], s_win[0], "n4", 1)
+        fetch(V, at_n5[0], s_win[0], "n5", 0)
+        fetch(V, at_n5[0], s_win[0], "n5", 1)
+        s_out(S, 2)
+        fetch(S, at_n4[1], s_win[1], "n4", 0)
+        fetch(S, at_n4[1], s_win[1], "n4", 1)
+        fetch(V, at_n5[1], s_win[1], "n5", 0)
+        fetch(V, at_n5[1], s_win[1], "n5", 1)
+        finish(0, slice(0, N))
+        s_out(S, 3)
+        fetch(S, at_n4[2], s_win[2], "n4", 0)
+        fetch(S, at_n4[2], s_win[2], "n4", 1)
+        fetch(V, at_n5[2], s_win[2], "n5", 0)
+        fetch(S, at_n5[2], s_win[2], "n5", 1)
+        finish(1, slice(0, N))
+        fetch(S, at_n4[3], s_win[3], "n4", 0)
+        fetch(V, at_n5[3], s_win[3], "n5", 0)
+        finish(2, slice(0, N))
+        fetch(S, at_n4[3], s_win[3], "n4", 1)
+        fetch(S, at_n5[3], s_win[3], "n5", 1)
+        finish(3, cols(0))
+        finish(3, cols(1))

@@ -46,9 +46,13 @@ def tile_picked_hkqtwicpkindgover_none_p_kernel(tc, x_words, x_scales, w1, w2, t
             nc.sync.dma_start(lists[name][:], src)
 
         def cols(h):
+            if h is None:
+                return slice(0, N)
             return slice(h * HALF, (h + 1) * HALF)
 
         def look(window, name, h):
+            if h is None:
+                return window[:].indirect(lists[name][:])
             return window[:].indirect(lists[name][:, h * (LIST_COLS // 2) : (h + 1) * (LIST_COLS // 2)])
 
         def fetch(engine, dst, window, name, h):
@@ -86,12 +90,12 @@ def tile_picked_hkqtwicpkindgover_none_p_kernel(tc, x_words, x_scales, w1, w2, t
 
         warm_in = sb("warm_in", [P, 1], F32)
         warm_out = sb("warm_out", [P, 1], F32)
-        nc.vector.memset(warm_in[:], 0.0)
+        nc.gpsimd.memset(warm_in[:], 0.0)
         nc.scalar.activation(warm_out[:], warm_in[:], ACT.Sigmoid)
 
         scale_table = sb("scale_table", [P, T], U8)
         table_i32 = scale_table[:].bitcast(I32)
-        nc.gpsimd.memset(table_i32, 0)
+        nc.vector.memset(table_i32, 0)
         scale_rows = x_scales[0].bitcast(I32)
 
         def load_scales():
@@ -104,10 +108,10 @@ def tile_picked_hkqtwicpkindgover_none_p_kernel(tc, x_words, x_scales, w1, w2, t
         ga_raw = sb("ga_raw", [P, 4], F32)
         gb_raw = sb("gb_raw", [P, 4], F32)
         w1_raw = sb("w1_raw", [P, 4, N], F32)
-        tabs = four("tab", [P, N], F32)
+        tabs = four("tab", [P, 2 * N], F32)
 
         def load_tab(t):
-            nc.sync.dma_start(tabs[t][:], dealt(tab)[t])
+            nc.sync.dma_start(tabs[t][:, 0:N], dealt(tab)[t])
 
         def load_w(dst, w):
             nc.sync.dma_start(dst[:], w.rearrange("(p j) c -> p j c", j=4))
@@ -156,17 +160,17 @@ def tile_picked_hkqtwicpkindgover_none_p_kernel(tc, x_words, x_scales, w1, w2, t
         offs_words = sb("offs_words", [P, N], U32)
         w2_grouped = pairs("w2_grouped")
         w1_grouped = pairs("w1_grouped")
-        z_grouped = pairs("z_grouped")
-        b_win = four("b_win", [P, N], F32)
-        a_win = four("a_win", [P, N], F32)
+        z_grouped = four("z_grouped", [P, N], BF16)
+        b_win = four("b_win", [P, 2 * N], F32)
+        a_win = four("a_win", [P, 2 * N], F32)
         gate = four("gate", [P, N], F32)
-        st_win = four("st_win", [P, N], F32)
+        st_win = four("st_win", [P, 2 * N], F32)
         st_far = four("st_far", [P, N], F32)
         kind_term = sb("kind_term", [P, 4, N], F32)
         far_term = sb("far_term", [P, 4, N], F32)
         larger = sb("larger", [P, 4, N], F32)
         z2_grouped = sb("z2_grouped", [P, N, 4], BF16)
-        s_win = four("s_win", [P, N], F32)
+        s_win = four("s_win", [P, 2 * N], F32)
         at_n4 = four("at_n4", [P, N], F32)
         at_n5 = four("at_n5", [P, N], F32)
         top = four("top", [P, N], F32)
@@ -189,41 +193,48 @@ def tile_picked_hkqtwicpkindgover_none_p_kernel(tc, x_words, x_scales, w1, w2, t
             acc["a", t] = product("bank%d" % (4 + t), quantise("w1_%d" % t, w1_grouped[t // 2][:, t % 2, :], P), (offs_words, offs_scales))
 
         def s_product(t):
-            acc["s", t] = product("bank%d" % t, quantise("z_%d" % t, z_grouped[t // 2][:, t % 2, :], P), q["z2"])
+            acc["s", t] = product("bank%d" % t, quantise("z_%d" % t, z_grouped[t][:], P), q["z2"])
 
         def b_out(engine, t):
             if engine == "vector":
-                nc.vector.tensor_scalar(b_win[t][:], acc["b", t][:], gb_half[:, t : t + 1], None, ALU.mult)
+                nc.vector.tensor_scalar(b_win[t][:, 0:N], acc["b", t][:], gb_half[:, t : t + 1], None, ALU.mult)
             else:
-                nc.scalar.activation(b_win[t][:], acc["b", t][:], ACT.Copy, scale=gb_half[:, t : t + 1])
+                nc.scalar.activation(b_win[t][:, 0:N], acc["b", t][:], ACT.Copy, scale=gb_half[:, t : t + 1])
 
         def far_b(t):
-            for h in range(2):
+            for h in (None,):
                 nc.scalar.activation(far_term[:, t, cols(h)], look(b_win[t], "n3", h), ACT.Copy, scale=-0.5)
 
         def kind_b(t):
-            for h in range(2):
+            for h in (None,):
                 nc.vector.tensor_tensor(kind_term[:, t, cols(h)], look(tabs[t], "n2", h), b_win[t][:, cols(h)], ALU.mult)
 
         def a_out(engine, t):
             if engine == "vector":
-                nc.vector.tensor_copy(a_win[t][:], acc["a", t][:])
+                nc.vector.tensor_copy(a_win[t][:, 0:N], acc["a", t][:])
             else:
-                nc.scalar.copy(a_win[t][:], acc["a", t][:])
+                nc.scalar.copy(a_win[t][:, 0:N], acc["a", t][:])
 
         def gate_a(t):
-            for h in range(2):
+            for h in (None,):
                 nc.scalar.activation(gate[t][:, cols(h)], look(a_win[t], "n1", h), ACT.Sigmoid)
 
         def gated(t):
-            nc.vector.scalar_tensor_tensor(st_win[t][:], acc["a", t][:], ga_half[:, t : t + 1], gate[t][:], ALU.mult, ALU.mult)
+            nc.vector.scalar_tensor_tensor(st_win[t][:, 0:N], acc["a", t][:], ga_half[:, t : t + 1], gate[t][:], ALU.mult, ALU.mult)
 
         def far_st(engines, t):
-            for h in range(2):
-                fetch(engines[h], st_far[t], st_win[t], "n1", h)
+            fetch(engines[0], st_far[t], st_win[t], "n1", None)
 
         def take_larger(t):
-            nc.vector.tensor_tensor(larger[:, t, :], st_win[t][:], st_far[t][:], ALU.max)
+            nc.vector.tensor_tensor(larger[:, t, :], st_win[t][:, 0:N], st_far[t][:], ALU.max)
+
+        def deal_z(engine, t):
+            o = z_grouped[t][:].rearrange("p (q c i j) -> p q c j i", q=16, c=4, i=2, j=4)
+            s = larger[:].rearrange("p j (q t c i) -> p t q c j i", q=16, t=4, c=4, i=2)[:, t]
+            if engine == "vector":
+                nc.vector.tensor_copy(o, s)
+            else:
+                nc.scalar.copy(o, s)
 
         def z2_sum(h):
             nc.vector.tensor_tensor(
@@ -238,14 +249,14 @@ def tile_picked_hkqtwicpkindgover_none_p_kernel(tc, x_words, x_scales, w1, w2, t
 
         def s_out(engine, t):
             if engine == "vector":
-                nc.vector.tensor_scalar(s_win[t][:], acc["s", t][:], 0.25, None, ALU.mult)
+                nc.vector.tensor_scalar(s_win[t][:, 0:N], acc["s", t][:], 0.25, None, ALU.mult)
             else:
-                nc.scalar.activation(s_win[t][:], acc["s", t][:], ACT.Copy, scale=0.25)
+                nc.scalar.activation(s_win[t][:, 0:N], acc["s", t][:], ACT.Copy, scale=0.25)
 
         def finish(t, c):
             nc.vector.tensor_tensor(top[t][:, c], at_n4[t][:, c], at_n5[t][:, c], ALU.max)
             nc.vector.scalar_tensor_tensor(result[t][:, c], s_win[t][:, c], -0.75, top[t][:, c], ALU.mult, ALU.add)
-            nc.sync.dma_start(dealt(out)[t][:, c], result[t][:, c])
+            nc.sync.dma_start(out.rearrange("(q t r) v -> t q r v", t=4, r=8)[t][:, :, c], result[t][:, c])
 
         V, S = "vector", "scalar"
         gather_packed(two_scales, scale_table, "two")
@@ -303,29 +314,25 @@ def tile_picked_hkqtwicpkindgover_none_p_kernel(tc, x_words, x_scales, w1, w2, t
         take_larger(2)
         far_st((S, S), 3)
         take_larger(3)
-        deal_copy(V, z_grouped[0][:], larger, 0)
-        deal_copy(S, z_grouped[1][:], larger, 1)
+        deal_z(V, 0)
+        deal_z(S, 1)
+        deal_z(V, 2)
+        deal_z(S, 3)
         s_product(0)
         s_product(1)
         s_product(2)
         s_product(3)
         s_out(S, 0)
         s_out(V, 1)
-        fetch(S, at_n4[0], s_win[0], "n4", 0)
-        fetch(S, at_n4[0], s_win[0], "n4", 1)
-        fetch(V, at_n5[0], s_win[0], "n5", 0)
-        fetch(V, at_n5[0], s_win[0], "n5", 1)
-        s_out(S, 2)
-        fetch(S, at_n4[1], s_win[1], "n4", 0)
-        fetch(S, at_n4[1], s_win[1], "n4", 1)
-        fetch(V, at_n5[1], s_win[1], "n5", 0)
-        fetch(V, at_n5[1], s_win[1], "n5", 1)
+        fetch(S, at_n4[0], s_win[0], "n4", None)
+        fetch(V, at_n5[0], s_win[0], "n5", None)
+        s_out(V, 2)
+        fetch(S, at_n4[1], s_win[1], "n4", None)
+        fetch(S, at_n5[1], s_win[1], "n5", None)
         finish(0, slice(0, N))
         s_out(S, 3)
-        fetch(S, at_n4[2], s_win[2], "n4", 0)
-        fetch(S, at_n4[2], s_win[2], "n4", 1)
-        fetch(V, at_n5[2], s_win[2], "n5", 0)
-        fetch(S, at_n5[2], s_win[2], "n5", 1)
+        fetch(S, at_n4[2], s_win[2], "n4", None)
+        fetch(V, at_n5[2], s_win[2], "n5", None)
         finish(1, slice(0, N))
         fetch(S, at_n4[3], s_win[3], "n4", 0)
         fetch(V, at_n5[3], s_win[3], "n5", 0)

@@ -2,7 +2,6 @@ from contextlib import ExitStack
 
 import concourse.mybir as mybir
 
-T = 2048
 FLOPS = 3 * 2 * 512 * 512 * 512
 
 F32 = mybir.dt.float32
@@ -16,28 +15,35 @@ ALU = mybir.AluOpType
 ACT = mybir.ActivationFunctionType
 
 P = 128
+TOKENS = 2048
 N = 512
-HALF = N // 2
+TILES = 4
+LAST = TILES - 1
 LIST_COLS = N // 16
+ALL = slice(0, N)
+HALVES = (slice(0, N // 2), slice(N // 2, N))
+
+B_TILES_ON_SCALAR = 1
+ST_TILES_ON_VECTOR = 1
+N5_TILES_ON_VECTOR = 3
 
 
-def tile_picked_hkqtwicpkindgover_none_p_kernel(tc, x_words, x_scales, w1, w2, tab, ga, gb, offs, two, n1, n2, n3, n4, n5, out):
+def tile_picked_hkqtwicpkindgover_none_p_kernel(
+    tc, x_words, x_scales, w1, w2, tab, ga, gb, offs, two, n1, n2, n3, n4, n5, out
+):
     nc = tc.nc
     with ExitStack() as ctx:
         held = ctx.enter_context(tc.tile_pool(name="held", bufs=1))
         psum = ctx.enter_context(tc.psum_pool(name="psum", bufs=1))
 
-        def sb(name, shape, dtype):
+        def sbuf(name, shape, dtype):
             return held.tile(shape, dtype, name=name, align_bytes=64)
 
-        def four(name, shape, dtype):
-            return [sb("%s%d" % (name, t), shape, dtype) for t in range(4)]
+        def sbufs(name, count, shape, dtype):
+            return [sbuf("%s%d" % (name, i), shape, dtype) for i in range(count)]
 
-        def pairs(name):
-            return [sb("%s%d" % (name, u), [P, 2, N], BF16) for u in range(2)]
-
-        def dealt(rows):
-            return rows.rearrange("(p t) c -> t p c", t=4)
+        def windows(name):
+            return sbufs(name, TILES, [P, 2 * N], F32)
 
         lists = {}
 
@@ -45,38 +51,36 @@ def tile_picked_hkqtwicpkindgover_none_p_kernel(tc, x_words, x_scales, w1, w2, t
             lists[name] = held.tile([P, LIST_COLS], U16, name="list_" + name)
             nc.sync.dma_start(lists[name][:], src)
 
-        def cols(h):
-            if h is None:
-                return slice(0, N)
-            return slice(h * HALF, (h + 1) * HALF)
+        def looked_up(table, name, cols):
+            return table[:].indirect(lists[name][:, cols.start // 16 : cols.stop // 16])
 
-        def look(window, name, h):
-            if h is None:
-                return window[:].indirect(lists[name][:])
-            return window[:].indirect(lists[name][:, h * (LIST_COLS // 2) : (h + 1) * (LIST_COLS // 2)])
-
-        def fetch(engine, dst, window, name, h):
-            if engine == "vector":
-                nc.vector.tensor_copy(dst[:, cols(h)], look(window, name, h))
+        def fetch(on_vector, dst, table, name, cols):
+            if on_vector:
+                nc.vector.tensor_copy(dst[:, cols], looked_up(table, name, cols))
             else:
-                nc.scalar.activation(dst[:, cols(h)], look(window, name, h), ACT.Copy)
+                nc.scalar.activation(dst[:, cols], looked_up(table, name, cols), ACT.Copy)
 
-        def deal_copy(engine, dst, src, u):
-            o = dst.rearrange("p e (m j) -> p m j e", j=4)
-            s = src[:].rearrange("p j (m u e) -> p u m j e", u=2, e=2)[:, u]
-            if engine == "vector":
-                nc.vector.tensor_copy(o, s)
+        def copy(on_vector, dst, src):
+            if on_vector:
+                nc.vector.tensor_copy(dst, src)
             else:
-                nc.scalar.copy(o, s)
+                nc.scalar.copy(dst, src)
 
-        def quantise(name, grouped, width):
-            codes = sb(name + "_codes", [P, width], U32)
-            scales = sb(name + "_scales", [P, width], U8)
-            nc.vector.quantize_mx(out=codes[:].bitcast(FP8X4), scales=scales[:], in_=grouped)
-            return codes, scales
+        def scaled_out_of_psum(on_vector, dst, acc, factor):
+            if on_vector:
+                nc.vector.tensor_scalar(dst, acc[:], factor, None, ALU.mult)
+            else:
+                nc.scalar.activation(dst, acc[:], ACT.Copy, scale=factor)
+
+        def quantise(name, grouped):
+            width = grouped.shape[1] // TILES
+            words = sbuf(name + "_words", [P, width], U32)
+            scales = sbuf(name + "_scales", [P, width], U8)
+            nc.vector.quantize_mx(out=words[:].bitcast(FP8X4), scales=scales[:], in_=grouped)
+            return words, scales
 
         def product(bank, stationary, moving):
-            acc = psum.tile([P, N], F32, name=bank, tag=bank)
+            acc = psum.tile([P, N], F32, name="bank%d" % bank, tag="bank%d" % bank)
             nc.tensor.matmul_mx(
                 out=acc[:],
                 lhsT=stationary[0][:].bitcast(FP8X4),
@@ -88,256 +92,150 @@ def tile_picked_hkqtwicpkindgover_none_p_kernel(tc, x_words, x_scales, w1, w2, t
             )
             return acc
 
-        warm_in = sb("warm_in", [P, 1], F32)
-        warm_out = sb("warm_out", [P, 1], F32)
+        def deal_weights(on_vector, grouped, raw, u):
+            copy(
+                on_vector,
+                grouped.rearrange("p e (m j) -> p m j e", j=TILES),
+                raw[:].rearrange("p j (m u e) -> p u m j e", u=2, e=2)[:, u],
+            )
+
+        warm_in = sbuf("warm_in", [P, 1], F32)
+        warm_out = sbuf("warm_out", [P, 1], F32)
         nc.gpsimd.memset(warm_in[:], 0.0)
         nc.scalar.activation(warm_out[:], warm_in[:], ACT.Sigmoid)
 
-        scale_table = sb("scale_table", [P, T], U8)
-        table_i32 = scale_table[:].bitcast(I32)
-        nc.vector.memset(table_i32, 0)
-        scale_rows = x_scales[0].bitcast(I32)
-
-        def load_scales():
-            nc.sync.dma_start(table_i32[0:P:8, :], scale_rows)
-            for r in (1, 2, 3):
-                nc.sync.dma_start(table_i32[r:P:32, :], scale_rows[r:16:4, :])
-
-        word_table = sb("word_table", [P, T], U32)
-        w2_raw = [sb("w2_raw%d" % h, [P, 4, HALF], F32) for h in range(2)]
-        ga_raw = sb("ga_raw", [P, 4], F32)
-        gb_raw = sb("gb_raw", [P, 4], F32)
-        w1_raw = sb("w1_raw", [P, 4, N], F32)
-        tabs = four("tab", [P, 2 * N], F32)
-
-        def load_tab(t):
-            nc.sync.dma_start(tabs[t][:, 0:N], dealt(tab)[t])
-
-        def load_w(dst, w):
-            nc.sync.dma_start(dst[:], w.rearrange("(p j) c -> p j c", j=4))
-
-        def load_w2():
-            for h in range(2):
-                load_w(w2_raw[h], w2[:, cols(h)])
-
-        def load_gains():
-            nc.sync.dma_start(ga_raw[:], ga.rearrange("(p t) o -> p (t o)", t=4))
-            nc.sync.dma_start(gb_raw[:], gb.rearrange("(p t) o -> p (t o)", t=4))
-
-        def load_words():
-            nc.sync.dma_start(word_table[:].bitcast(I32), x_words[0].rearrange("p c r -> p (c r)").bitcast(I32))
-
         load_list("two", two)
         load_list("offs", offs)
-        load_scales()
-        load_words()
-        load_gains()
-        load_w2()
+
+        scale_table = sbuf("scale_table", [P, TOKENS], U8)
+        scale_table_i32 = scale_table[:].bitcast(I32)
+        scale_rows = x_scales[0].bitcast(I32)
+        nc.vector.memset(scale_table_i32, 0)
+        nc.sync.dma_start(scale_table_i32[0:P:8, :], scale_rows)
+        for r in range(1, 4):
+            nc.sync.dma_start(scale_table_i32[r:P:32, :], scale_rows[r:16:4, :])
+
+        word_table = sbuf("word_table", [P, TOKENS], U32)
+        nc.sync.dma_start(word_table[:].bitcast(I32), x_words[0].rearrange("p c r -> p (c r)").bitcast(I32))
+
+        ga_raw = sbuf("ga_raw", [P, TILES], F32)
+        gb_raw = sbuf("gb_raw", [P, TILES], F32)
+        nc.sync.dma_start(ga_raw[:], ga.rearrange("(p t) o -> p (t o)", t=TILES))
+        nc.sync.dma_start(gb_raw[:], gb.rearrange("(p t) o -> p (t o)", t=TILES))
+
+        w2_raw = sbufs("w2_raw", 2, [P, TILES, N // 2], F32)
+        for half, cols in enumerate(HALVES):
+            nc.sync.dma_start(w2_raw[half][:], w2[:, cols].rearrange("(p j) c -> p j c", j=TILES))
         load_list("n3", n3)
-        load_w(w1_raw, w1)
+        w1_raw = sbuf("w1_raw", [P, TILES, N], F32)
+        nc.sync.dma_start(w1_raw[:], w1.rearrange("(p j) c -> p j c", j=TILES))
         load_list("n2", n2)
-        load_tab(0)
-        load_tab(1)
-        load_list("n1", n1)
-        load_tab(2)
-        load_tab(3)
+        tab_win = windows("tab_win")
+        tab_dealt = tab.rearrange("(p t) c -> t p c", t=TILES)
+        for t in range(TILES):
+            nc.sync.dma_start(tab_win[t][:, ALL], tab_dealt[t])
+            if t == TILES // 2 - 1:
+                load_list("n1", n1)
         load_list("n4", n4)
         load_list("n5", n5)
 
-        half_sign = sb("half_sign", [P, 4], F32)
-        ga_half = sb("ga_half", [P, 4], F32)
-        gb_half = sb("gb_half", [P, 4], F32)
+        two_scales = sbuf("two_scales", [P, N], U8)
+        offs_bytes = sbuf("offs_bytes", [P, N], U8)
+        nc.vector.tensor_copy(offs_bytes[:], looked_up(scale_table, "offs", ALL))
+        nc.vector.tensor_copy(two_scales[:], looked_up(scale_table, "two", ALL))
+        offs_scales = sbuf("offs_scales", [P, N], U8)
+        nc.vector.tensor_copy(offs_scales[:].bitcast(I32), offs_bytes[:].bitcast(I32))
+        for r in range(2, 4):
+            nc.scalar.dma_start(offs_scales[:].bitcast(I32)[r:P:32, :], offs_bytes[:].bitcast(I32)[8 * r : P : 32, :])
 
-        def signs():
-            nc.vector.tensor_scalar(half_sign[:], ga_raw[:], 0.0, -0.5, ALU.is_ge, ALU.add)
-            nc.vector.tensor_tensor(gb_half[:], gb_raw[:], half_sign[:], ALU.mult)
-            nc.vector.tensor_tensor(ga_half[:], ga_raw[:], half_sign[:], ALU.mult)
+        h = sbuf("h", [P, TILES], F32)
+        h_gb = sbuf("h_gb", [P, TILES], F32)
+        h_ga = sbuf("h_ga", [P, TILES], F32)
+        nc.gpsimd.tensor_scalar(h[:], ga_raw[:], 0.0, -0.5, ALU.is_ge, ALU.add)
+        nc.gpsimd.tensor_tensor(h_gb[:], gb_raw[:], h[:], ALU.mult)
+        nc.gpsimd.tensor_tensor(h_ga[:], ga_raw[:], h[:], ALU.mult)
 
-        two_scales = sb("two_scales", [P, N], U8)
-        offs_bytes = sb("offs_bytes", [P, N], U8)
-        offs_scales = sb("offs_scales", [P, N], U8)
-        two_words = sb("two_words", [P, N], U32)
-        offs_words = sb("offs_words", [P, N], U32)
-        w2_grouped = pairs("w2_grouped")
-        w1_grouped = pairs("w1_grouped")
-        z_grouped = four("z_grouped", [P, N], BF16)
-        b_win = four("b_win", [P, 2 * N], F32)
-        a_win = four("a_win", [P, 2 * N], F32)
-        gate = four("gate", [P, N], F32)
-        st_win = four("st_win", [P, 2 * N], F32)
-        st_far = four("st_far", [P, N], F32)
-        kind_term = sb("kind_term", [P, 4, N], F32)
-        far_term = sb("far_term", [P, 4, N], F32)
-        larger = sb("larger", [P, 4, N], F32)
-        z2_grouped = sb("z2_grouped", [P, N, 4], BF16)
-        s_win = four("s_win", [P, 2 * N], F32)
-        at_n4 = four("at_n4", [P, N], F32)
-        at_n5 = four("at_n5", [P, N], F32)
-        top = four("top", [P, N], F32)
-        result = four("result", [P, N], F32)
-        acc = {}
-        q = {}
+        two_words = sbuf("two_words", [P, N], U32)
+        offs_words = sbuf("offs_words", [P, N], U32)
+        nc.vector.tensor_copy(two_words[:], looked_up(word_table, "two", ALL))
+        nc.vector.tensor_copy(offs_words[:], looked_up(word_table, "offs", ALL))
 
-        def gather_packed(dst, table, name):
-            nc.vector.tensor_copy(dst[:], table[:].indirect(lists[name][:]))
+        w2_grouped = sbufs("w2_grouped", 2, [P, 2, N], BF16)
+        for half, cols in enumerate(HALVES):
+            for u in range(2):
+                deal_weights(False, w2_grouped[u][:, :, cols], w2_raw[half], u)
+        b_acc = [
+            product(t, quantise("w2_%d" % t, w2_grouped[t // 2][:, t % 2, :]), (two_words, two_scales))
+            for t in range(TILES)
+        ]
+        b_win = windows("b_win")
+        for t in range(TILES):
+            scaled_out_of_psum(t >= B_TILES_ON_SCALAR, b_win[t][:, ALL], b_acc[t], h_gb[:, t : t + 1])
 
-        def place_scales():
-            nc.vector.tensor_copy(offs_scales[:].bitcast(I32), offs_bytes[:].bitcast(I32))
-            for r in (2, 3):
-                nc.scalar.dma_start(offs_scales[:].bitcast(I32)[r:P:32, :], offs_bytes[:].bitcast(I32)[8 * r : P : 32, :])
+        w1_grouped = sbufs("w1_grouped", 2, [P, 2, N], BF16)
+        for u in range(2):
+            deal_weights(True, w1_grouped[u][:], w1_raw, u)
+        a_acc = [
+            product(TILES + t, quantise("w1_%d" % t, w1_grouped[t // 2][:, t % 2, :]), (offs_words, offs_scales))
+            for t in range(TILES)
+        ]
 
-        def b_product(t):
-            acc["b", t] = product("bank%d" % t, quantise("w2_%d" % t, w2_grouped[t // 2][:, t % 2, :], P), (two_words, two_scales))
+        query_term = sbuf("query_term", [P, TILES, N], F32)
+        kind_term = sbuf("kind_term", [P, TILES, N], F32)
+        for t in range(TILES):
+            nc.scalar.activation(query_term[:, t, :], looked_up(b_win[t], "n3", ALL), ACT.Copy, scale=-0.5)
+        for t in range(TILES):
+            nc.vector.tensor_tensor(kind_term[:, t, :], looked_up(tab_win[t], "n2", ALL), b_win[t][:, ALL], ALU.mult)
 
-        def a_product(t):
-            acc["a", t] = product("bank%d" % (4 + t), quantise("w1_%d" % t, w1_grouped[t // 2][:, t % 2, :], P), (offs_words, offs_scales))
+        a_win = windows("a_win")
+        gate = sbufs("gate", TILES, [P, N], F32)
+        for t in range(TILES):
+            nc.scalar.copy(a_win[t][:, ALL], a_acc[t][:])
+            nc.scalar.activation(gate[t][:], looked_up(a_win[t], "n1", ALL), ACT.Sigmoid)
 
-        def s_product(t):
-            acc["s", t] = product("bank%d" % t, quantise("z_%d" % t, z_grouped[t][:], P), q["z2"])
-
-        def b_out(engine, t):
-            if engine == "vector":
-                nc.vector.tensor_scalar(b_win[t][:, 0:N], acc["b", t][:], gb_half[:, t : t + 1], None, ALU.mult)
-            else:
-                nc.scalar.activation(b_win[t][:, 0:N], acc["b", t][:], ACT.Copy, scale=gb_half[:, t : t + 1])
-
-        def far_b(t):
-            for h in (None,):
-                nc.scalar.activation(far_term[:, t, cols(h)], look(b_win[t], "n3", h), ACT.Copy, scale=-0.5)
-
-        def kind_b(t):
-            for h in (None,):
-                nc.vector.tensor_tensor(kind_term[:, t, cols(h)], look(tabs[t], "n2", h), b_win[t][:, cols(h)], ALU.mult)
-
-        def a_out(engine, t):
-            if engine == "vector":
-                nc.vector.tensor_copy(a_win[t][:, 0:N], acc["a", t][:])
-            else:
-                nc.scalar.copy(a_win[t][:, 0:N], acc["a", t][:])
-
-        def gate_a(t):
-            for h in (None,):
-                nc.scalar.activation(gate[t][:, cols(h)], look(a_win[t], "n1", h), ACT.Sigmoid)
-
-        def gated(t):
-            nc.vector.scalar_tensor_tensor(st_win[t][:, 0:N], acc["a", t][:], ga_half[:, t : t + 1], gate[t][:], ALU.mult, ALU.mult)
-
-        def far_st(engines, t):
-            fetch(engines[0], st_far[t], st_win[t], "n1", None)
-
-        def take_larger(t):
-            nc.vector.tensor_tensor(larger[:, t, :], st_win[t][:, 0:N], st_far[t][:], ALU.max)
-
-        def deal_z(engine, t):
-            o = z_grouped[t][:].rearrange("p (q c i j) -> p q c j i", q=16, c=4, i=2, j=4)
-            s = larger[:].rearrange("p j (q t c i) -> p t q c j i", q=16, t=4, c=4, i=2)[:, t]
-            if engine == "vector":
-                nc.vector.tensor_copy(o, s)
-            else:
-                nc.scalar.copy(o, s)
-
-        def z2_sum(h):
+        z2_grouped = sbuf("z2_grouped", [P, N, TILES], BF16)
+        for cols in HALVES:
             nc.vector.tensor_tensor(
-                z2_grouped[:, cols(h), :].rearrange("p (c i) t -> p c t i", i=2),
-                kind_term[:, :, cols(h)].rearrange("p t (c i) -> p c t i", i=2),
-                far_term[:, :, cols(h)].rearrange("p t (c i) -> p c t i", i=2),
+                z2_grouped[:, cols, :].rearrange("p (c i) t -> p c t i", i=2),
+                kind_term[:, :, cols].rearrange("p t (c i) -> p c t i", i=2),
+                query_term[:, :, cols].rearrange("p t (c i) -> p c t i", i=2),
                 ALU.add,
             )
+        z2_packed = quantise("z2", z2_grouped[:].rearrange("p c t -> p (c t)"))
 
-        def z2_quantise():
-            q["z2"] = quantise("z2", z2_grouped[:].rearrange("p c t -> p (c t)"), N)
+        st_win = windows("st_win")
+        st_at_n1 = sbufs("st_at_n1", TILES, [P, N], F32)
+        z = sbuf("z", [P, TILES, N], F32)
+        for t in range(TILES):
+            nc.vector.scalar_tensor_tensor(st_win[t][:, ALL], a_acc[t][:], h_ga[:, t : t + 1], gate[t][:], ALU.mult, ALU.mult)
+        for t in range(TILES):
+            fetch(t < ST_TILES_ON_VECTOR, st_at_n1[t], st_win[t], "n1", ALL)
+        for t in range(TILES):
+            nc.vector.tensor_tensor(z[:, t, :], st_win[t][:, ALL], st_at_n1[t][:], ALU.max)
 
-        def s_out(engine, t):
-            if engine == "vector":
-                nc.vector.tensor_scalar(s_win[t][:, 0:N], acc["s", t][:], 0.25, None, ALU.mult)
-            else:
-                nc.scalar.activation(s_win[t][:, 0:N], acc["s", t][:], ACT.Copy, scale=0.25)
+        z_grouped = sbufs("z_grouped", TILES, [P, N], BF16)
+        for t in range(TILES):
+            copy(
+                t % 2 == 0,
+                z_grouped[t][:].rearrange("p (q c i j) -> p q c j i", c=4, i=2, j=TILES),
+                z[:].rearrange("p j (q t c i) -> p t q c j i", t=TILES, c=4, i=2)[:, t],
+            )
+        s_acc = [product(t, quantise("z_%d" % t, z_grouped[t][:]), z2_packed) for t in range(TILES)]
 
-        def finish(t, c):
-            nc.vector.tensor_tensor(top[t][:, c], at_n4[t][:, c], at_n5[t][:, c], ALU.max)
-            nc.vector.scalar_tensor_tensor(result[t][:, c], s_win[t][:, c], -0.75, top[t][:, c], ALU.mult, ALU.add)
-            nc.sync.dma_start(out.rearrange("(q t r) v -> t q r v", t=4, r=8)[t][:, :, c], result[t][:, c])
-
-        V, S = "vector", "scalar"
-        gather_packed(two_scales, scale_table, "two")
-        gather_packed(offs_bytes, scale_table, "offs")
-        place_scales()
-        signs()
-        gather_packed(two_words, word_table, "two")
-        gather_packed(offs_words, word_table, "offs")
-        deal_copy(S, w2_grouped[0][:, :, cols(0)], w2_raw[0], 0)
-        deal_copy(S, w2_grouped[1][:, :, cols(0)], w2_raw[0], 1)
-        deal_copy(S, w2_grouped[0][:, :, cols(1)], w2_raw[1], 0)
-        deal_copy(S, w2_grouped[1][:, :, cols(1)], w2_raw[1], 1)
-        b_product(0)
-        b_product(1)
-        b_product(2)
-        b_product(3)
-        b_out(S, 0)
-        b_out(V, 1)
-        b_out(V, 2)
-        b_out(V, 3)
-        deal_copy(V, w1_grouped[0][:], w1_raw, 0)
-        deal_copy(V, w1_grouped[1][:], w1_raw, 1)
-        a_product(0)
-        a_product(1)
-        a_product(2)
-        a_product(3)
-        far_b(0)
-        far_b(1)
-        far_b(2)
-        far_b(3)
-        kind_b(0)
-        kind_b(1)
-        kind_b(2)
-        kind_b(3)
-        a_out(S, 0)
-        gate_a(0)
-        a_out(S, 1)
-        gate_a(1)
-        a_out(S, 2)
-        gate_a(2)
-        a_out(S, 3)
-        gate_a(3)
-        gated(0)
-        gated(1)
-        z2_sum(0)
-        z2_sum(1)
-        gated(2)
-        z2_quantise()
-        far_st((V, V), 0)
-        gated(3)
-        take_larger(0)
-        far_st((S, S), 1)
-        take_larger(1)
-        far_st((S, S), 2)
-        take_larger(2)
-        far_st((S, S), 3)
-        take_larger(3)
-        deal_z(V, 0)
-        deal_z(S, 1)
-        deal_z(V, 2)
-        deal_z(S, 3)
-        s_product(0)
-        s_product(1)
-        s_product(2)
-        s_product(3)
-        s_out(S, 0)
-        s_out(V, 1)
-        fetch(S, at_n4[0], s_win[0], "n4", None)
-        fetch(V, at_n5[0], s_win[0], "n5", None)
-        s_out(V, 2)
-        fetch(S, at_n4[1], s_win[1], "n4", None)
-        fetch(S, at_n5[1], s_win[1], "n5", None)
-        finish(0, slice(0, N))
-        s_out(S, 3)
-        fetch(S, at_n4[2], s_win[2], "n4", None)
-        fetch(V, at_n5[2], s_win[2], "n5", None)
-        finish(1, slice(0, N))
-        fetch(S, at_n4[3], s_win[3], "n4", 0)
-        fetch(V, at_n5[3], s_win[3], "n5", 0)
-        finish(2, slice(0, N))
-        fetch(S, at_n4[3], s_win[3], "n4", 1)
-        fetch(S, at_n5[3], s_win[3], "n5", 1)
-        finish(3, cols(0))
-        finish(3, cols(1))
+        s_win = windows("s_win")
+        s_at_n4 = sbufs("s_at_n4", TILES, [P, N], F32)
+        s_at_n5 = sbufs("s_at_n5", TILES, [P, N], F32)
+        larger = sbufs("larger", TILES, [P, N], F32)
+        result = sbufs("result", TILES, [P, N], F32)
+        out_dealt = out.rearrange("(q t r) v -> t q r v", t=TILES, r=8)
+        for t in range(TILES):
+            nc.scalar.activation(s_win[t][:, ALL], s_acc[t][:], ACT.Copy, scale=0.25)
+        for t in range(TILES):
+            for cols in HALVES if t == LAST else (ALL,):
+                fetch(False, s_at_n4[t], s_win[t], "n4", cols)
+                fetch(t < N5_TILES_ON_VECTOR, s_at_n5[t], s_win[t], "n5", cols)
+                nc.vector.tensor_tensor(larger[t][:, cols], s_at_n4[t][:, cols], s_at_n5[t][:, cols], ALU.max)
+                nc.vector.scalar_tensor_tensor(
+                    result[t][:, cols], s_win[t][:, cols], -0.75, larger[t][:, cols], ALU.mult, ALU.add
+                )
+                nc.sync.dma_start(out_dealt[t][:, :, cols], result[t][:, cols])

@@ -23,7 +23,7 @@ LIST_COLS = N // 16
 ALL = slice(0, N)
 HALVES = (slice(0, N // 2), slice(N // 2, N))
 
-B_TILES_ON_SCALAR = 1
+B_TILES_ON_SCALAR = 2
 ST_TILES_ON_VECTOR = 1
 N5_TILES_ON_VECTOR = 3
 
@@ -77,16 +77,16 @@ def tile_picked_hkqtwicpkindgover_none_p_kernel(
             words = sbuf(name + "_words", [P, width], U32)
             scales = sbuf(name + "_scales", [P, width], U8)
             nc.vector.quantize_mx(out=words[:].bitcast(FP8X4), scales=scales[:], in_=grouped)
-            return words, scales
+            return words[:], scales[:]
 
         def product(bank, stationary, moving):
             acc = psum.tile([P, N], F32, name="bank%d" % bank, tag="bank%d" % bank)
             nc.tensor.matmul_mx(
                 out=acc[:],
-                lhsT=stationary[0][:].bitcast(FP8X4),
-                lhsT_scale=stationary[1][:],
-                rhs=moving[0][:].bitcast(FP8X4),
-                rhs_scale=moving[1][:],
+                lhsT=stationary[0].bitcast(FP8X4),
+                lhsT_scale=stationary[1],
+                rhs=moving[0].bitcast(FP8X4),
+                rhs_scale=moving[1],
                 start=True,
                 stop=True,
             )
@@ -165,7 +165,7 @@ def tile_picked_hkqtwicpkindgover_none_p_kernel(
             for u in range(2):
                 deal_weights(False, w2_grouped[u][:, :, cols], w2_raw[half], u)
         b_acc = [
-            product(t, quantise("w2_%d" % t, w2_grouped[t // 2][:, t % 2, :]), (two_words, two_scales))
+            product(t, quantise("w2_%d" % t, w2_grouped[t // 2][:, t % 2, :]), (two_words[:], two_scales[:]))
             for t in range(TILES)
         ]
         b_win = windows("b_win")
@@ -175,10 +175,12 @@ def tile_picked_hkqtwicpkindgover_none_p_kernel(
         w1_grouped = sbufs("w1_grouped", 2, [P, 2, N], BF16)
         for u in range(2):
             deal_weights(True, w1_grouped[u][:], w1_raw, u)
-        a_acc = [
-            product(TILES + t, quantise("w1_%d" % t, w1_grouped[t // 2][:, t % 2, :]), (offs_words, offs_scales))
-            for t in range(TILES)
-        ]
+        a_acc = []
+        for u in range(2):
+            words, scales = quantise("w1_%d" % u, w1_grouped[u][:].rearrange("p e c -> p (e c)"))
+            for e in range(2):
+                own = slice(e * P, (e + 1) * P)
+                a_acc.append(product(TILES + 2 * u + e, (words[:, own], scales[:, own]), (offs_words[:], offs_scales[:])))
 
         query_term = sbuf("query_term", [P, TILES, N], F32)
         kind_term = sbuf("kind_term", [P, TILES, N], F32)
@@ -196,9 +198,9 @@ def tile_picked_hkqtwicpkindgover_none_p_kernel(
         z2_grouped = sbuf("z2_grouped", [P, N, TILES], BF16)
         for cols in HALVES:
             nc.vector.tensor_tensor(
-                z2_grouped[:, cols, :].rearrange("p (c i) t -> p c t i", i=2),
-                kind_term[:, :, cols].rearrange("p t (c i) -> p c t i", i=2),
-                query_term[:, :, cols].rearrange("p t (c i) -> p c t i", i=2),
+                z2_grouped[:, cols, :].rearrange("p (c i) t -> p c t i", i=4),
+                kind_term[:, :, cols].rearrange("p t (c i) -> p c t i", i=4),
+                query_term[:, :, cols].rearrange("p t (c i) -> p c t i", i=4),
                 ALU.add,
             )
         z2_packed = quantise("z2", z2_grouped[:].rearrange("p c t -> p (c t)"))

from contextlib import ExitStack

import concourse.mybir as mybir

FLOPS = 3 * 2 * 512 * 512 * 512

F32 = mybir.dt.float32
BF16 = mybir.dt.bfloat16
I32 = mybir.dt.int32
U32 = mybir.dt.uint32
U16 = mybir.dt.uint16
U8 = mybir.dt.uint8
FP8X4 = mybir.dt.float8_e4m3fn_x4
ALU = mybir.AluOpType
ACT = mybir.ActivationFunctionType

P = 128
TOKENS = 2048
N = 512
TILES = 4
LAST = TILES - 1
LIST_COLS = N // 16
ALL = slice(0, N)
HALVES = (slice(0, N // 2), slice(N // 2, N))

B_TILES_ON_SCALAR = 2
ST_TILES_ON_VECTOR = 1
N5_TILES_ON_VECTOR = 3


def tile_picked_hkqtwicpkindgover_none_p_kernel(
    tc, x_words, x_scales, w1, w2, tab, ga, gb, offs, two, n1, n2, n3, n4, n5, out
):
    nc = tc.nc
    with ExitStack() as ctx:
        held = ctx.enter_context(tc.tile_pool(name="held", bufs=1))
        psum = ctx.enter_context(tc.psum_pool(name="psum", bufs=1))

        def sbuf(name, shape, dtype):
            return held.tile(shape, dtype, name=name, align_bytes=64)

        def sbufs(name, count, shape, dtype):
            return [sbuf("%s%d" % (name, i), shape, dtype) for i in range(count)]

        def windows(name):
            return sbufs(name, TILES, [P, 2 * N], F32)

        lists = {}

        def load_list(name, src):
            lists[name] = held.tile([P, LIST_COLS], U16, name="list_" + name)
            nc.sync.dma_start(lists[name][:], src)

        def looked_up(table, name, cols):
            return table[:].indirect(lists[name][:, cols.start // 16 : cols.stop // 16])

        def fetch(on_vector, dst, table, name, cols):
            if on_vector:
                nc.vector.tensor_copy(dst[:, cols], looked_up(table, name, cols))
            else:
                nc.scalar.activation(dst[:, cols], looked_up(table, name, cols), ACT.Copy)

        def copy(on_vector, dst, src):
            if on_vector:
                nc.vector.tensor_copy(dst, src)
            else:
                nc.scalar.copy(dst, src)

        def scaled_out_of_psum(on_vector, dst, acc, factor):
            if on_vector:
                nc.vector.tensor_scalar(dst, acc[:], factor, None, ALU.mult)
            else:
                nc.scalar.activation(dst, acc[:], ACT.Copy, scale=factor)

        def quantise(name, grouped):
            width = grouped.shape[1] // TILES
            words = sbuf(name + "_words", [P, width], U32)
            scales = sbuf(name + "_scales", [P, width], U8)
            nc.vector.quantize_mx(out=words[:].bitcast(FP8X4), scales=scales[:], in_=grouped)
            return words[:], scales[:]

        def product(bank, stationary, moving):
            acc = psum.tile([P, N], F32, name="bank%d" % bank, tag="bank%d" % bank)
            nc.tensor.matmul_mx(
                out=acc[:],
                lhsT=stationary[0].bitcast(FP8X4),
                lhsT_scale=stationary[1],
                rhs=moving[0].bitcast(FP8X4),
                rhs_scale=moving[1],
                start=True,
                stop=True,
            )
            return acc

        def deal_weights(on_vector, grouped, raw, u):
            copy(
                on_vector,
                grouped.rearrange("p e (m j) -> p m j e", j=TILES),
                raw[:].rearrange("p j (m u e) -> p u m j e", u=2, e=2)[:, u],
            )

        warm_in = sbuf("warm_in", [P, 1], F32)
        warm_out = sbuf("warm_out", [P, 1], F32)
        nc.gpsimd.memset(warm_in[:], 0.0)
        nc.scalar.activation(warm_out[:], warm_in[:], ACT.Sigmoid)

        load_list("two", two)
        load_list("offs", offs)

        scale_table = sbuf("scale_table", [P, TOKENS], U8)
        scale_table_i32 = scale_table[:].bitcast(I32)
        scale_rows = x_scales[0].bitcast(I32)
        nc.vector.memset(scale_table_i32, 0)
        nc.sync.dma_start(scale_table_i32[0:P:8, :], scale_rows)
        for r in range(1, 4):
            nc.sync.dma_start(scale_table_i32[r:P:32, :], scale_rows[r:16:4, :])

        word_table = sbuf("word_table", [P, TOKENS], U32)
        nc.sync.dma_start(word_table[:].bitcast(I32), x_words[0].rearrange("p c r -> p (c r)").bitcast(I32))

        ga_raw = sbuf("ga_raw", [P, TILES], F32)
        gb_raw = sbuf("gb_raw", [P, TILES], F32)
        nc.sync.dma_start(ga_raw[:], ga.rearrange("(p t) o -> p (t o)", t=TILES))
        nc.sync.dma_start(gb_raw[:], gb.rearrange("(p t) o -> p (t o)", t=TILES))

        w2_raw = sbufs("w2_raw", 2, [P, TILES, N // 2], F32)
        for half, cols in enumerate(HALVES):
            nc.sync.dma_start(w2_raw[half][:], w2[:, cols].rearrange("(p j) c -> p j c", j=TILES))
        load_list("n3", n3)
        w1_raw = sbuf("w1_raw", [P, TILES, N], F32)
        nc.sync.dma_start(w1_raw[:], w1.rearrange("(p j) c -> p j c", j=TILES))
        load_list("n2", n2)
        tab_win = windows("tab_win")
        tab_dealt = tab.rearrange("(p t) c -> t p c", t=TILES)
        for t in range(TILES):
            nc.sync.dma_start(tab_win[t][:, ALL], tab_dealt[t])
            if t == TILES // 2 - 1:
                load_list("n1", n1)
        load_list("n4", n4)
        load_list("n5", n5)

        two_scales = sbuf("two_scales", [P, N], U8)
        offs_bytes = sbuf("offs_bytes", [P, N], U8)
        nc.vector.tensor_copy(offs_bytes[:], looked_up(scale_table, "offs", ALL))
        nc.vector.tensor_copy(two_scales[:], looked_up(scale_table, "two", ALL))
        offs_scales = sbuf("offs_scales", [P, N], U8)
        nc.vector.tensor_copy(offs_scales[:].bitcast(I32), offs_bytes[:].bitcast(I32))
        for r in range(2, 4):
            nc.scalar.dma_start(offs_scales[:].bitcast(I32)[r:P:32, :], offs_bytes[:].bitcast(I32)[8 * r : P : 32, :])

        h = sbuf("h", [P, TILES], F32)
        h_gb = sbuf("h_gb", [P, TILES], F32)
        h_ga = sbuf("h_ga", [P, TILES], F32)
        nc.gpsimd.tensor_scalar(h[:], ga_raw[:], 0.0, -0.5, ALU.is_ge, ALU.add)
        nc.gpsimd.tensor_tensor(h_gb[:], gb_raw[:], h[:], ALU.mult)
        nc.gpsimd.tensor_tensor(h_ga[:], ga_raw[:], h[:], ALU.mult)

        two_words = sbuf("two_words", [P, N], U32)
        offs_words = sbuf("offs_words", [P, N], U32)
        nc.vector.tensor_copy(two_words[:], looked_up(word_table, "two", ALL))
        nc.vector.tensor_copy(offs_words[:], looked_up(word_table, "offs", ALL))

        w2_grouped = sbufs("w2_grouped", 2, [P, 2, N], BF16)
        for half, cols in enumerate(HALVES):
            for u in range(2):
                deal_weights(False, w2_grouped[u][:, :, cols], w2_raw[half], u)
        b_acc = [
            product(t, quantise("w2_%d" % t, w2_grouped[t // 2][:, t % 2, :]), (two_words[:], two_scales[:]))
            for t in range(TILES)
        ]
        b_win = windows("b_win")
        for t in range(TILES):
            scaled_out_of_psum(t >= B_TILES_ON_SCALAR, b_win[t][:, ALL], b_acc[t], h_gb[:, t : t + 1])

        w1_grouped = sbufs("w1_grouped", 2, [P, 2, N], BF16)
        for u in range(2):
            deal_weights(True, w1_grouped[u][:], w1_raw, u)
        a_acc = []
        for u in range(2):
            words, scales = quantise("w1_%d" % u, w1_grouped[u][:].rearrange("p e c -> p (e c)"))
            for e in range(2):
                own = slice(e * P, (e + 1) * P)
                a_acc.append(product(TILES + 2 * u + e, (words[:, own], scales[:, own]), (offs_words[:], offs_scales[:])))

        query_term = sbuf("query_term", [P, TILES, N], F32)
        kind_term = sbuf("kind_term", [P, TILES, N], F32)
        for t in range(TILES):
            nc.scalar.activation(query_term[:, t, :], looked_up(b_win[t], "n3", ALL), ACT.Copy, scale=-0.5)
        for t in range(TILES):
            nc.vector.tensor_tensor(kind_term[:, t, :], looked_up(tab_win[t], "n2", ALL), b_win[t][:, ALL], ALU.mult)

        a_win = windows("a_win")
        gate = sbufs("gate", TILES, [P, N], F32)
        for t in range(TILES):
            nc.scalar.copy(a_win[t][:, ALL], a_acc[t][:])
            nc.scalar.activation(gate[t][:], looked_up(a_win[t], "n1", ALL), ACT.Sigmoid)

        z2_grouped = sbuf("z2_grouped", [P, N, TILES], BF16)
        for cols in HALVES:
            nc.vector.tensor_tensor(
                z2_grouped[:, cols, :].rearrange("p (c i) t -> p c t i", i=4),
                kind_term[:, :, cols].rearrange("p t (c i) -> p c t i", i=4),
                query_term[:, :, cols].rearrange("p t (c i) -> p c t i", i=4),
                ALU.add,
            )
        z2_packed = quantise("z2", z2_grouped[:].rearrange("p c t -> p (c t)"))

        st_win = windows("st_win")
        st_at_n1 = sbufs("st_at_n1", TILES, [P, N], F32)
        z = sbuf("z", [P, TILES, N], F32)
        for t in range(TILES):
            nc.vector.scalar_tensor_tensor(st_win[t][:, ALL], a_acc[t][:], h_ga[:, t : t + 1], gate[t][:], ALU.mult, ALU.mult)
        for t in range(TILES):
            fetch(t < ST_TILES_ON_VECTOR, st_at_n1[t], st_win[t], "n1", ALL)
        for t in range(TILES):
            nc.vector.tensor_tensor(z[:, t, :], st_win[t][:, ALL], st_at_n1[t][:], ALU.max)

        z_grouped = sbufs("z_grouped", TILES, [P, N], BF16)
        for t in range(TILES):
            copy(
                t % 2 == 0,
                z_grouped[t][:].rearrange("p (q c i j) -> p q c j i", c=4, i=2, j=TILES),
                z[:].rearrange("p j (q t c i) -> p t q c j i", t=TILES, c=4, i=2)[:, t],
            )
        s_acc = [product(t, quantise("z_%d" % t, z_grouped[t][:]), z2_packed) for t in range(TILES)]

        s_win = windows("s_win")
        s_at_n4 = sbufs("s_at_n4", TILES, [P, N], F32)
        s_at_n5 = sbufs("s_at_n5", TILES, [P, N], F32)
        larger = sbufs("larger", TILES, [P, N], F32)
        result = sbufs("result", TILES, [P, N], F32)
        out_dealt = out.rearrange("(q t r) v -> t q r v", t=TILES, r=8)
        for t in range(TILES):
            nc.scalar.activation(s_win[t][:, ALL], s_acc[t][:], ACT.Copy, scale=0.25)
        for t in range(TILES):
            for cols in HALVES if t == LAST else (ALL,):
                fetch(False, s_at_n4[t], s_win[t], "n4", cols)
                fetch(t < N5_TILES_ON_VECTOR, s_at_n5[t], s_win[t], "n5", cols)
                nc.vector.tensor_tensor(larger[t][:, cols], s_at_n4[t][:, cols], s_at_n5[t][:, cols], ALU.max)
                nc.vector.scalar_tensor_tensor(
                    result[t][:, cols], s_win[t][:, cols], -0.75, larger[t][:, cols], ALU.mult, ALU.add
                )
                nc.sync.dma_start(out_dealt[t][:, :, cols], result[t][:, cols])
